import numpy as np
import ml_dtypes


def mxq(x, axis, fmt="e4m3"):
    dtype, down = {"e4m3": (ml_dtypes.float8_e4m3fn, 7), "e5m2": (ml_dtypes.float8_e5m2, 14)}[fmt]
    v = np.moveaxis(np.asarray(x, np.float32).astype(ml_dtypes.bfloat16).astype(np.float64), axis, -1)
    blocks = v.reshape(v.shape[:-1] + (-1, 32))
    amax = np.abs(blocks).max(-1, keepdims=True)
    byte = np.maximum(np.where(amax > 0, np.frexp(amax)[1] - 1 + 127, 0) - down, 1)
    scale = np.exp2(byte - 127.0)
    codes = (blocks / scale).astype(np.float32).astype(dtype).astype(np.float64)
    return np.moveaxis((codes * scale).reshape(v.shape), -1, axis)


WIDE = False


def mx_kscale(k):
    if not WIDE:
        return np.ones(k)
    levels = np.array([10, -10, 5, -5, 0])
    if k % 512:
        return np.exp2(np.random.permutation(np.resize(levels, k // 32))).repeat(32)
    a = np.empty((k // 512, 16))
    for p in range(k // 512):
        a[p, :8] = np.random.permutation(np.resize(levels, 8))
        for g in range(8):
            far = levels[np.abs(levels - a[p, g]) >= 10]
            a[p, g + 8] = far[np.random.randint(len(far))]
    return np.exp2(a.ravel()).repeat(32)


def f64(x):
    return np.asarray(x).astype(np.float64)


def striped(idx):
    return np.tile(np.asarray(idx).reshape(-1, 16).T, (8, 1)).astype(np.uint16)


def unstriped(offs):
    return offs[:16].T.reshape(-1).astype(np.int64)


E2M1 = np.array([0.0, 0.5, 1.0, 1.5, 2.0, 3.0, 4.0, 6.0, -0.0, -0.5, -1.0, -1.5, -2.0, -3.0, -4.0, -6.0])


def pack_weight(w, fmt):
    k, n = w.shape
    w = f64(np.asarray(w, np.float32).astype(ml_dtypes.bfloat16)).reshape(k // 32, 32, n)
    amax = np.abs(w).max(1)
    if fmt == "e4m3":
        byte = np.frexp(amax)[1] - 1 + 127 - 7
    else:
        mant, ex = np.frexp(amax / 6.0)
        byte = np.where(mant > 0.5, ex, ex - 1) + 127
    byte = np.clip(np.where(amax > 0, byte, 1), 1, 254)
    scaled = (w * np.exp2(127.0 - byte)[:, None, :]).reshape(k, n).astype(np.float32)
    by_word = np.ascontiguousarray(scaled.reshape(k // 512, 128, 4, n).transpose(0, 1, 3, 2))
    if fmt == "e4m3":
        words = by_word.astype(ml_dtypes.float8_e4m3fn).view(np.uint8)
    else:
        c = by_word.astype(ml_dtypes.float4_e2m1fn).view(np.uint8) & 0xF
        words = (c[..., 0::2] | (c[..., 1::2] << 4)).reshape(k // 512, 128, 2 * n)
    return np.ascontiguousarray(words), np.ascontiguousarray(byte.astype(np.uint8).reshape(k // 512, 16, n))


def unpack_weight(words, scales, fmt):
    g, _, n = scales.shape
    words = np.ascontiguousarray(words).reshape(g, 128, n, -1)
    if fmt == "e4m3":
        vals = words.view(ml_dtypes.float8_e4m3fn).astype(np.float64)
    else:
        nib = np.empty((g, 128, n, 4), np.uint8)
        nib[..., 0::2] = words & 0xF
        nib[..., 1::2] = words >> 4
        vals = E2M1[nib]
    vals = vals * np.repeat(np.exp2(scales.astype(np.float64) - 127.0), 8, axis=1)[..., None]
    return vals.transpose(0, 1, 3, 2).reshape(g * 512, n)


D, E, T, I, Q, G = 512, 512, 2048, 512, 512, 64


def setup_inputs():
    n = np.random.standard_normal
    idx = np.random.permutation(T)[:I]
    fd = mx_kscale(D)
    fe = mx_kscale(E)
    keysp = pack_weight(n((D, T)) / fd[:, None], "e4m3")
    valsp = pack_weight(n((E, T)) / fe[:, None], "e4m3")
    return {
        "query": (n((D, Q)) * 0.7 / np.sqrt(D) * fd[:, None]).astype(np.float32),
        "keys_words": keysp[0],
        "keys_scales": keysp[1],
        "lse": (np.random.uniform(6.2, 6.5, (1, Q))).astype(np.float32),
        "mult": (np.random.uniform(20.0, 120.0, (1, Q))).astype(np.float32),
        "gout": (n((E, Q)) * 1 / np.sqrt(E) * fe[:, None]).astype(np.float32),
        "vals_words": valsp[0],
        "vals_scales": valsp[1],
        "old": (np.random.uniform(0.0, 8.0, (I, G))).astype(np.float32),
        "fade": (np.random.uniform(0.5, 1.0, (I, 1))).astype(np.float32),
        "offs": striped(idx),
    }


def reference(query, keys_words, keys_scales, lse, mult, gout, vals_words, vals_scales, old, fade, offs):
    idx = unstriped(offs)
    keysu = unpack_weight(keys_words, keys_scales, "e4m3")
    valsu = unpack_weight(vals_words, vals_scales, "e4m3")
    keysidxg = keysu[:, idx]
    queryq = mxq(f64(query), 0, "e4m3")
    a = keysidxg.T @ queryq
    valsidxg = valsu[:, idx]
    goutq = mxq(f64(gout), 0, "e4m3")
    dp = valsidxg.T @ goutq
    p = np.exp(a - f64(lse))
    cv = p * (1.0 - p * f64(mult)) * np.square(dp) * 512.0
    y = cv.reshape(I, G, Q // G).sum(axis=2) + f64(old) * f64(fade)
    return y

@@ -1,0 +1,205 @@
+from contextlib import ExitStack
+
+import concourse.mybir as mybir
+from concourse.masks import make_identity
+
+D, T, SLOTS, Q, GROUPS = 512, 2048, 512, 512, 64
+FLOPS = 2 * 2 * D * SLOTS * Q
+
+F32 = mybir.dt.float32
+BF16 = mybir.dt.bfloat16
+I32 = mybir.dt.int32
+U32 = mybir.dt.uint32
+U16 = mybir.dt.uint16
+U8 = mybir.dt.uint8
+FP8X4 = mybir.dt.float8_e4m3fn_x4
+ACT = mybir.ActivationFunctionType
+MULT = mybir.AluOpType.mult
+ADD = mybir.AluOpType.add
+
+P = 128
+PACK = 4
+TILES = Q // P
+BLOCKS = SLOTS // P
+HALF = SLOTS // 2
+VALS_SCALE_ROW = 4
+
+
+def tile_attend_curvatures_kernel(
+    tc, query, keys_words, keys_scales, lse, mult, gout, vals_words, vals_scales, old, fade, offs, out
+):
+    nc = tc.nc
+    with ExitStack() as ctx:
+        keep = ctx.enter_context(tc.tile_pool(name="keep", bufs=1))
+        psum = ctx.enter_context(tc.psum_pool(name="psum", bufs=1))
+
+        offsets = keep.tile([P, SLOTS // 16], U16, name="offsets")
+        nc.sync.dma_start(offsets[:], offs)
+        lse_cols = keep.tile([P, TILES], F32, name="lse_cols")
+        nc.sync.dma_start(lse_cols[:], lse.rearrange("o (p j) -> (o p) j", j=TILES))
+        mult_cols = keep.tile([P, TILES], F32, name="mult_cols")
+        nc.sync.dma_start(mult_cols[:], mult.rearrange("o (p j) -> (o p) j", j=TILES))
+
+        def load_scale_rows(name, scales, first_row, zero_engine, queue):
+            pool_rows = keep.tile([P, T], U8, name=name, align_bytes=64)
+            zero_engine.memset(pool_rows[:].bitcast(I32), 0)
+            rows = scales[0].bitcast(I32).rearrange("(quad r) c -> r quad c", r=4)
+            for r in range(4):
+                queue.dma_start(pool_rows[first_row + r : P : 32, :].bitcast(I32), rows[r])
+            return pool_rows
+
+        def load_words(name, words):
+            pool_words = keep.tile([P, T], I32, name=name, align_bytes=64)
+            nc.sync.dma_start(pool_words[:], words[0].rearrange("p n t -> p (n t)").bitcast(I32))
+            return pool_words
+
+        def load_rows(name, matrix, c0, c1):
+            raw = keep.tile([P, PACK, c1 - c0], F32, name=name, tag=name)
+            nc.sync.dma_start(raw[:], matrix[:, c0:c1].rearrange("(p t) q -> p t q", t=PACK))
+            return raw
+
+        key_scale_pool = load_scale_rows("key_scale_pool", keys_scales, 0, nc.vector, nc.sync)
+        query_raw = load_rows("query_raw", query, 0, Q)
+        val_scale_pool = load_scale_rows("val_scale_pool", vals_scales, VALS_SCALE_ROW, nc.gpsimd, nc.sync)
+        gout_raw0 = load_rows("gout_raw0", gout, 0, Q // 2)
+        key_pool = load_words("key_pool", keys_words)
+        gout_raw1 = load_rows("gout_raw1", gout, Q // 2, Q)
+        val_pool = load_words("val_pool", vals_words)
+
+        neg_lse = keep.tile([P, TILES], F32, name="neg_lse")
+        nc.gpsimd.tensor_scalar(neg_lse[:], lse_cols[:], -1.0, 0.0, MULT, ADD)
+        slope = keep.tile([P, TILES], F32, name="slope")
+        nc.gpsimd.tensor_scalar(slope[:], mult_cols[:], -512.0, 0.0, MULT, ADD)
+        identity = keep.tile([P, P], F32, name="identity")
+        make_identity(nc, identity[:])
+
+        def interleave(copy, woven, raw, j0, j1, m0, m1):
+            copy(
+                woven[:, j0:j1, m0:m1, :].rearrange("p j m t -> p m t j"),
+                raw[:].rearrange("p t (m j) -> p m t j", j=TILES)[:, :, :, j0:j1],
+            )
+
+        def gather(gathered, pool_ap, s0, s1):
+            nc.vector.tensor_copy(gathered[:, s0:s1], pool_ap.indirect(offsets[:, s0 // 16 : s1 // 16]))
+
+        key_scales = keep.tile([P, SLOTS], U8, name="key_scales", align_bytes=64)
+        gather(key_scales, key_scale_pool[:], 0, SLOTS)
+
+        query_woven = keep.tile([P, TILES, P, PACK], BF16, name="query_woven", align_bytes=64)
+        interleave(nc.vector.tensor_copy, query_woven, query_raw, 0, 2, 0, P)
+        interleave(nc.scalar.copy, query_woven, query_raw, 2, 4, 0, P)
+
+        val_scales = keep.tile([P, SLOTS], U8, name="val_scales", align_bytes=64)
+        gather(val_scales, val_scale_pool[:], 0, SLOTS)
+
+        def quantize(name, woven):
+            codes = keep.tile([P, Q], U32, name=name + "_codes", align_bytes=64)
+            scales = keep.tile([P, Q], U8, name=name + "_scales", align_bytes=64)
+            nc.vector.quantize_mx(
+                out=codes[:].bitcast(FP8X4), scales=scales[:], in_=woven[:].rearrange("p j m t -> p (j m t)")
+            )
+            return codes, scales
+
+        query_codes, query_scales = quantize("query", query_woven)
+
+        gout_woven = keep.tile([P, TILES, P, PACK], BF16, name="gout_woven", align_bytes=64)
+        for j0 in (0, 2):
+            interleave(nc.scalar.copy, gout_woven, gout_raw0, j0, j0 + 2, 0, P // 2)
+
+        old_rows = keep.tile([P, BLOCKS, GROUPS], F32, name="old_rows")
+        nc.sync.dma_start(old_rows[:], old.rearrange("(b p) g -> p b g", p=P))
+        fade_cols = keep.tile([P, BLOCKS], F32, name="fade_cols")
+        with nc.allow_non_contiguous_dma(reason="one value of fade for each partition and block"):
+            nc.sync.dma_start(fade_cols[:], fade.rearrange("(b p) o -> p (b o)", p=P))
+
+        keys = keep.tile([P, SLOTS], U32, name="keys", align_bytes=64)
+        weight = keep.tile([P, BLOCKS, TILES, P], F32, name="weight")
+        damping = keep.tile([P, BLOCKS, TILES, P], F32, name="damping")
+        damped = keep.tile([P, BLOCKS, TILES, P], F32, name="damped")
+        for h in range(2):
+            gather(keys, key_pool[:].bitcast(U32), h * HALF, (h + 1) * HALF)
+        for j0 in (0, 2):
+            interleave(nc.vector.tensor_copy, gout_woven, gout_raw1, j0, j0 + 2, P // 2, P)
+        gout_codes, gout_scales = quantize("gout", gout_woven)
+
+        for h in range(2):
+            slots = slice(h * HALF, (h + 1) * HALF)
+            blocks = slice(2 * h, 2 * h + 2)
+            for jj in range(2):
+                scores = psum.tile([P, 2, HALF], F32, name="scores", tag="early", bufs=4)
+                for j1 in range(2):
+                    cols = slice((2 * jj + j1) * P, (2 * jj + j1 + 1) * P)
+                    nc.tensor.matmul_mx(
+                        scores[:, j1, :],
+                        lhsT=query_codes[:, cols].bitcast(FP8X4),
+                        lhsT_scale=query_scales[:, cols],
+                        rhs=keys[:, slots].bitcast(FP8X4),
+                        rhs_scale=key_scales[:, slots],
+                        start=True,
+                        stop=True,
+                    )
+                for j1 in range(2):
+                    j = 2 * jj + j1
+                    nc.scalar.activation(
+                        weight[:, blocks, j, :],
+                        scores[:, j1, :].rearrange("p (b s) -> p b s", s=P),
+                        ACT.Exp,
+                        bias=neg_lse[:, j : j + 1],
+                    )
+            for j in range(TILES):
+                nc.scalar.activation(
+                    damping[:, blocks, j, :], weight[:, blocks, j, :], ACT.Copy, bias=512.0, scale=slope[:, j : j + 1]
+                )
+            if h == 0:
+                for b in range(2):
+                    nc.vector.tensor_tensor(damped[:, b], weight[:, b], damping[:, b], MULT)
+
+        vals = keep.tile([P, SLOTS], U32, name="vals", align_bytes=64)
+        for h in range(2):
+            gather(vals, val_pool[:].bitcast(U32), h * HALF, (h + 1) * HALF)
+
+        squares = []
+        for b in range(BLOCKS):
+            slots = slice(b * P, (b + 1) * P)
+            grads = psum.tile([P, TILES, P], F32, name="grads", tag="grads", bufs=4)
+            for j in range(TILES):
+                cols = slice(j * P, (j + 1) * P)
+                nc.tensor.matmul_mx(
+                    grads[:, j, :],
+                    lhsT=gout_codes[:, cols].bitcast(FP8X4),
+                    lhsT_scale=gout_scales[:, cols],
+                    rhs=vals[:, slots].bitcast(FP8X4),
+                    rhs_scale=val_scales[VALS_SCALE_ROW:P, slots],
+                    start=True,
+                    stop=True,
+                )
+            square = keep.tile([P, TILES, P], F32, name="square", tag="square", bufs=4)
+            nc.scalar.activation(square[:], grads[:], ACT.Square)
+            squares.append(square)
+
+        sums = []
+
+        def finish(b):
+            pairs = sums[b][:].rearrange("p (g h) -> p h g", h=2)
+            partial = keep.tile([P, GROUPS], F32, name="partial", tag="partial", bufs=4)
+            nc.vector.scalar_tensor_tensor(
+                partial[:], old_rows[:, b, :], fade_cols[:, b : b + 1], pairs[:, 0, :], MULT, ADD
+            )
+            result = keep.tile([P, GROUPS], F32, name="result", tag="result", bufs=4)
+            nc.vector.tensor_tensor(result[:], pairs[:, 1, :], partial[:], ADD)
+            nc.sync.dma_start(out[b * P : (b + 1) * P, :], result[:])
+
+        for b in range(BLOCKS):
+            if b >= 2:
+                nc.vector.tensor_tensor(damped[:, b], weight[:, b], damping[:, b], MULT)
+            curvature = keep.tile([P, TILES, P], F32, name="curvature", tag="curvature", bufs=4)
+            nc.vector.tensor_tensor(curvature[:], damped[:, b], squares[b][:], MULT)
+            total = psum.tile([P, P], F32, name="total", tag="early", bufs=4)
+            for j in range(TILES):
+                nc.tensor.matmul(
+                    total[:], curvature[:, j, :], identity[:], start=(j == 0), stop=(j == TILES - 1), is_transpose=True
+                )
+            sums.append(total)
+            if b >= 1:
+                finish(b - 1)
+        finish(BLOCKS - 1)

@@ -35,21 +35,17 @@ def tile_attend_curvatures_kernel(
 
         offsets = keep.tile([P, SLOTS // 16], U16, name="offsets")
         nc.sync.dma_start(offsets[:], offs)
-        lse_cols = keep.tile([P, TILES], F32, name="lse_cols")
-        nc.sync.dma_start(lse_cols[:], lse.rearrange("o (p j) -> (o p) j", j=TILES))
-        mult_cols = keep.tile([P, TILES], F32, name="mult_cols")
-        nc.sync.dma_start(mult_cols[:], mult.rearrange("o (p j) -> (o p) j", j=TILES))
 
-        def load_scale_rows(name, scales, first_row, zero_engine, queue):
-            pool_rows = keep.tile([P, T], U8, name=name, align_bytes=64)
+        def load_scale_rows(name, scales, first_row, zero_engine, queues):
+            pool_rows = keep.tile([P, T], U8, name=name, tag=name, align_bytes=64)
             zero_engine.memset(pool_rows[:].bitcast(I32), 0)
             rows = scales[0].bitcast(I32).rearrange("(quad r) c -> r quad c", r=4)
-            for r in range(4):
+            for r, queue in enumerate(queues):
                 queue.dma_start(pool_rows[first_row + r : P : 32, :].bitcast(I32), rows[r])
             return pool_rows
 
         def load_words(name, words):
-            pool_words = keep.tile([P, T], I32, name=name, align_bytes=64)
+            pool_words = keep.tile([P, T], I32, name=name, tag=name, align_bytes=64)
             nc.sync.dma_start(pool_words[:], words[0].rearrange("p n t -> p (n t)").bitcast(I32))
             return pool_words
 
@@ -58,11 +54,17 @@ def tile_attend_curvatures_kernel(
             nc.sync.dma_start(raw[:], matrix[:, c0:c1].rearrange("(p t) q -> p t q", t=PACK))
             return raw
 
-        key_scale_pool = load_scale_rows("key_scale_pool", keys_scales, 0, nc.vector, nc.sync)
+        val_scale_pool = load_scale_rows(
+            "val_scale_pool", vals_scales, VALS_SCALE_ROW, nc.vector, [nc.gpsimd, nc.gpsimd, nc.scalar, nc.scalar]
+        )
         query_raw = load_rows("query_raw", query, 0, Q)
-        val_scale_pool = load_scale_rows("val_scale_pool", vals_scales, VALS_SCALE_ROW, nc.gpsimd, nc.sync)
-        gout_raw0 = load_rows("gout_raw0", gout, 0, Q // 2)
+        key_scale_pool = load_scale_rows("key_scale_pool", keys_scales, 0, nc.vector, [nc.sync] * 4)
         key_pool = load_words("key_pool", keys_words)
+        lse_cols = keep.tile([P, TILES], F32, name="lse_cols")
+        nc.sync.dma_start(lse_cols[:], lse.rearrange("o (p j) -> (o p) j", j=TILES))
+        mult_cols = keep.tile([P, TILES], F32, name="mult_cols")
+        nc.sync.dma_start(mult_cols[:], mult.rearrange("o (p j) -> (o p) j", j=TILES))
+        gout_raw0 = load_rows("gout_raw0", gout, 0, Q // 2)
         gout_raw1 = load_rows("gout_raw1", gout, Q // 2, Q)
         val_pool = load_words("val_pool", vals_words)
 
@@ -82,29 +84,27 @@ def tile_attend_curvatures_kernel(
         def gather(gathered, pool_ap, s0, s1):
             nc.vector.tensor_copy(gathered[:, s0:s1], pool_ap.indirect(offsets[:, s0 // 16 : s1 // 16]))
 
-        key_scales = keep.tile([P, SLOTS], U8, name="key_scales", align_bytes=64)
-        gather(key_scales, key_scale_pool[:], 0, SLOTS)
+        val_scales = keep.tile([P, SLOTS], U8, name="val_scales", align_bytes=64)
+        gather(val_scales, val_scale_pool[:], 0, SLOTS)
 
         query_woven = keep.tile([P, TILES, P, PACK], BF16, name="query_woven", align_bytes=64)
         interleave(nc.vector.tensor_copy, query_woven, query_raw, 0, 2, 0, P)
         interleave(nc.scalar.copy, query_woven, query_raw, 2, 4, 0, P)
 
-        val_scales = keep.tile([P, SLOTS], U8, name="val_scales", align_bytes=64)
-        gather(val_scales, val_scale_pool[:], 0, SLOTS)
+        key_scales = keep.tile([P, SLOTS], U8, name="key_scales", align_bytes=64)
+        gather(key_scales, key_scale_pool[:], 0, SLOTS)
 
-        def quantize(name, woven):
+        def quantize(name, woven, scale_tag):
             codes = keep.tile([P, Q], U32, name=name + "_codes", align_bytes=64)
-            scales = keep.tile([P, Q], U8, name=name + "_scales", align_bytes=64)
+            scales = keep.tile([P, Q], U8, name=name + "_scales", tag=scale_tag, align_bytes=64)
             nc.vector.quantize_mx(
                 out=codes[:].bitcast(FP8X4), scales=scales[:], in_=woven[:].rearrange("p j m t -> p (j m t)")
             )
             return codes, scales
 
-        query_codes, query_scales = quantize("query", query_woven)
+        query_codes, query_scales = quantize("query", query_woven, "key_scale_pool")
 
         gout_woven = keep.tile([P, TILES, P, PACK], BF16, name="gout_woven", align_bytes=64)
-        for j0 in (0, 2):
-            interleave(nc.scalar.copy, gout_woven, gout_raw0, j0, j0 + 2, 0, P // 2)
 
         old_rows = keep.tile([P, BLOCKS, GROUPS], F32, name="old_rows")
         nc.sync.dma_start(old_rows[:], old.rearrange("(b p) g -> p b g", p=P))
@@ -115,12 +115,14 @@ def tile_attend_curvatures_kernel(
         keys = keep.tile([P, SLOTS], U32, name="keys", align_bytes=64)
         weight = keep.tile([P, BLOCKS, TILES, P], F32, name="weight")
         damping = keep.tile([P, BLOCKS, TILES, P], F32, name="damping")
-        damped = keep.tile([P, BLOCKS, TILES, P], F32, name="damped")
+        damped_first = keep.tile([P, TILES, P], F32, name="damped_first")
         for h in range(2):
             gather(keys, key_pool[:].bitcast(U32), h * HALF, (h + 1) * HALF)
         for j0 in (0, 2):
+            interleave(nc.vector.tensor_copy, gout_woven, gout_raw0, j0, j0 + 2, 0, P // 2)
+        for j0 in (0, 2):
             interleave(nc.vector.tensor_copy, gout_woven, gout_raw1, j0, j0 + 2, P // 2, P)
-        gout_codes, gout_scales = quantize("gout", gout_woven)
+        gout_codes, gout_scales = quantize("gout", gout_woven, "gout_scales")
 
         for h in range(2):
             slots = slice(h * HALF, (h + 1) * HALF)
@@ -147,16 +149,29 @@ def tile_attend_curvatures_kernel(
                         bias=neg_lse[:, j : j + 1],
                     )
             for j in range(TILES):
-                nc.scalar.activation(
-                    damping[:, blocks, j, :], weight[:, blocks, j, :], ACT.Copy, bias=512.0, scale=slope[:, j : j + 1]
-                )
+                if h == 0 and j < 2:
+                    nc.vector.tensor_scalar(
+                        damping[:, blocks, j, :], weight[:, blocks, j, :], slope[:, j : j + 1], 512.0, MULT, ADD
+                    )
+                else:
+                    nc.scalar.activation(
+                        damping[:, blocks, j, :],
+                        weight[:, blocks, j, :],
+                        ACT.Copy,
+                        bias=512.0,
+                        scale=slope[:, j : j + 1],
+                    )
             if h == 0:
-                for b in range(2):
-                    nc.vector.tensor_tensor(damped[:, b], weight[:, b], damping[:, b], MULT)
+                nc.vector.tensor_tensor(damped_first[:], weight[:, 0], damping[:, 0], MULT)
 
         vals = keep.tile([P, SLOTS], U32, name="vals", align_bytes=64)
         for h in range(2):
             gather(vals, val_pool[:].bitcast(U32), h * HALF, (h + 1) * HALF)
+
+        damped_rest = keep.tile([P, BLOCKS - 1, TILES, P], F32, name="damped_rest", tag="val_pool", align_bytes=64)
+        damped = [damped_first[:]] + [damped_rest[:, b] for b in range(BLOCKS - 1)]
+        for b in range(1, BLOCKS):
+            nc.vector.tensor_tensor(damped[b], weight[:, b], damping[:, b], MULT)
 
         squares = []
         for b in range(BLOCKS):
@@ -190,10 +205,11 @@ def tile_attend_curvatures_kernel(
             nc.sync.dma_start(out[b * P : (b + 1) * P, :], result[:])
 
         for b in range(BLOCKS):
-            if b >= 2:
-                nc.vector.tensor_tensor(damped[:, b], weight[:, b], damping[:, b], MULT)
             curvature = keep.tile([P, TILES, P], F32, name="curvature", tag="curvature", bufs=4)
-            nc.vector.tensor_tensor(curvature[:], damped[:, b], squares[b][:], MULT)
+            step = TILES if b < BLOCKS - 1 else 1
+            for j in range(0, TILES, step):
+                tiles = slice(j, j + step)
+                nc.vector.tensor_tensor(curvature[:, tiles], damped[b][:, tiles], squares[b][:, tiles], MULT)
             total = psum.tile([P, P], F32, name="total", tag="early", bufs=4)
             for j in range(TILES):
                 nc.tensor.matmul(

@@ -35,6 +35,10 @@ def tile_attend_curvatures_kernel(
 
         offsets = keep.tile([P, SLOTS // 16], U16, name="offsets")
         nc.sync.dma_start(offsets[:], offs)
+        lse_cols = keep.tile([P, TILES], F32, name="lse_cols")
+        nc.sync.dma_start(lse_cols[:], lse.rearrange("o (p j) -> (o p) j", j=TILES))
+        mult_cols = keep.tile([P, TILES], F32, name="mult_cols")
+        nc.sync.dma_start(mult_cols[:], mult.rearrange("o (p j) -> (o p) j", j=TILES))
 
         def load_scale_rows(name, scales, first_row, zero_engine, queues):
             pool_rows = keep.tile([P, T], U8, name=name, tag=name, align_bytes=64)
@@ -54,16 +58,12 @@ def tile_attend_curvatures_kernel(
             nc.sync.dma_start(raw[:], matrix[:, c0:c1].rearrange("(p t) q -> p t q", t=PACK))
             return raw
 
-        val_scale_pool = load_scale_rows(
-            "val_scale_pool", vals_scales, VALS_SCALE_ROW, nc.vector, [nc.gpsimd, nc.gpsimd, nc.scalar, nc.scalar]
+        key_scale_pool = load_scale_rows(
+            "key_scale_pool", keys_scales, 0, nc.vector, [nc.sync, nc.sync, nc.scalar, nc.scalar]
         )
         query_raw = load_rows("query_raw", query, 0, Q)
-        key_scale_pool = load_scale_rows("key_scale_pool", keys_scales, 0, nc.vector, [nc.sync] * 4)
+        val_scale_pool = load_scale_rows("val_scale_pool", vals_scales, VALS_SCALE_ROW, nc.gpsimd, [nc.sync] * 4)
         key_pool = load_words("key_pool", keys_words)
-        lse_cols = keep.tile([P, TILES], F32, name="lse_cols")
-        nc.sync.dma_start(lse_cols[:], lse.rearrange("o (p j) -> (o p) j", j=TILES))
-        mult_cols = keep.tile([P, TILES], F32, name="mult_cols")
-        nc.sync.dma_start(mult_cols[:], mult.rearrange("o (p j) -> (o p) j", j=TILES))
         gout_raw0 = load_rows("gout_raw0", gout, 0, Q // 2)
         gout_raw1 = load_rows("gout_raw1", gout, Q // 2, Q)
         val_pool = load_words("val_pool", vals_words)
@@ -84,15 +84,15 @@ def tile_attend_curvatures_kernel(
         def gather(gathered, pool_ap, s0, s1):
             nc.vector.tensor_copy(gathered[:, s0:s1], pool_ap.indirect(offsets[:, s0 // 16 : s1 // 16]))
 
-        val_scales = keep.tile([P, SLOTS], U8, name="val_scales", align_bytes=64)
-        gather(val_scales, val_scale_pool[:], 0, SLOTS)
+        key_scales = keep.tile([P, SLOTS], U8, name="key_scales", align_bytes=64)
+        gather(key_scales, key_scale_pool[:], 0, SLOTS)
 
         query_woven = keep.tile([P, TILES, P, PACK], BF16, name="query_woven", align_bytes=64)
         interleave(nc.vector.tensor_copy, query_woven, query_raw, 0, 2, 0, P)
         interleave(nc.scalar.copy, query_woven, query_raw, 2, 4, 0, P)
 
-        key_scales = keep.tile([P, SLOTS], U8, name="key_scales", align_bytes=64)
-        gather(key_scales, key_scale_pool[:], 0, SLOTS)
+        val_scales = keep.tile([P, SLOTS], U8, name="val_scales", align_bytes=64)
+        gather(val_scales, val_scale_pool[:], 0, SLOTS)
 
         def quantize(name, woven, scale_tag):
             codes = keep.tile([P, Q], U32, name=name + "_codes", align_bytes=64)
@@ -102,7 +102,7 @@ def tile_attend_curvatures_kernel(
             )
             return codes, scales
 
-        query_codes, query_scales = quantize("query", query_woven, "key_scale_pool")
+        query_codes, query_scales = quantize("query", query_woven, "val_scale_pool")
 
         gout_woven = keep.tile([P, TILES, P, PACK], BF16, name="gout_woven", align_bytes=64)
 
@@ -113,109 +113,102 @@ def tile_attend_curvatures_kernel(
             nc.sync.dma_start(fade_cols[:], fade.rearrange("(b p) o -> p (b o)", p=P))
 
         keys = keep.tile([P, SLOTS], U32, name="keys", align_bytes=64)
-        weight = keep.tile([P, BLOCKS, TILES, P], F32, name="weight")
-        damping = keep.tile([P, BLOCKS, TILES, P], F32, name="damping")
-        damped_first = keep.tile([P, TILES, P], F32, name="damped_first")
         for h in range(2):
             gather(keys, key_pool[:].bitcast(U32), h * HALF, (h + 1) * HALF)
         for j0 in (0, 2):
             interleave(nc.vector.tensor_copy, gout_woven, gout_raw0, j0, j0 + 2, 0, P // 2)
         for j0 in (0, 2):
             interleave(nc.vector.tensor_copy, gout_woven, gout_raw1, j0, j0 + 2, P // 2, P)
-        gout_codes, gout_scales = quantize("gout", gout_woven, "gout_scales")
 
-        for h in range(2):
+        def multiply(tag, codes, scales, columns, column_scales, h, pair):
             slots = slice(h * HALF, (h + 1) * HALF)
-            blocks = slice(2 * h, 2 * h + 2)
-            for jj in range(2):
-                scores = psum.tile([P, 2, HALF], F32, name="scores", tag="early", bufs=4)
-                for j1 in range(2):
-                    cols = slice((2 * jj + j1) * P, (2 * jj + j1 + 1) * P)
-                    nc.tensor.matmul_mx(
-                        scores[:, j1, :],
-                        lhsT=query_codes[:, cols].bitcast(FP8X4),
-                        lhsT_scale=query_scales[:, cols],
-                        rhs=keys[:, slots].bitcast(FP8X4),
-                        rhs_scale=key_scales[:, slots],
-                        start=True,
-                        stop=True,
-                    )
-                for j1 in range(2):
-                    j = 2 * jj + j1
-                    nc.scalar.activation(
-                        weight[:, blocks, j, :],
-                        scores[:, j1, :].rearrange("p (b s) -> p b s", s=P),
-                        ACT.Exp,
-                        bias=neg_lse[:, j : j + 1],
-                    )
+            bank = psum.tile([P, 2, HALF], F32, name=tag, tag=tag, bufs=4)
+            for i in range(2):
+                rows = slice((2 * pair + i) * P, (2 * pair + i + 1) * P)
+                nc.tensor.matmul_mx(
+                    bank[:, i, :],
+                    lhsT=codes[:, rows].bitcast(FP8X4),
+                    lhsT_scale=scales[:, rows],
+                    rhs=columns[:, slots].bitcast(FP8X4),
+                    rhs_scale=column_scales[:, slots],
+                    start=True,
+                    stop=True,
+                )
+            return bank
+
+        parts = [(h, pair) for h in range(2) for pair in range(2)]
+        weight = keep.tile([P, 2, TILES, HALF], F32, name="weight")
+        damping = keep.tile([P, 2, TILES, HALF], F32, name="damping")
+        damping_first = keep.tile([P, 2, HALF], F32, name="damping_first", tag="gout_raw1")
+        damped_first = keep.tile([P, 2, HALF], F32, name="damped_first")
+        for h in range(2):
+            for pair in range(2):
+                scores = multiply("early", query_codes, query_scales, keys, key_scales[:], h, pair)
+                for i in range(2):
+                    j = 2 * pair + i
+                    nc.scalar.activation(weight[:, h, j, :], scores[:, i, :], ACT.Exp, bias=neg_lse[:, j : j + 1])
             for j in range(TILES):
                 if h == 0 and j < 2:
                     nc.vector.tensor_scalar(
-                        damping[:, blocks, j, :], weight[:, blocks, j, :], slope[:, j : j + 1], 512.0, MULT, ADD
+                        damping_first[:, j, :], weight[:, h, j, :], slope[:, j : j + 1], 512.0, MULT, ADD
                     )
                 else:
                     nc.scalar.activation(
-                        damping[:, blocks, j, :],
-                        weight[:, blocks, j, :],
-                        ACT.Copy,
-                        bias=512.0,
-                        scale=slope[:, j : j + 1],
+                        damping[:, h, j, :], weight[:, h, j, :], ACT.Copy, bias=512.0, scale=slope[:, j : j + 1]
                     )
             if h == 0:
-                nc.vector.tensor_tensor(damped_first[:], weight[:, 0], damping[:, 0], MULT)
+                gout_codes, gout_scales = quantize("gout", gout_woven, "gout_scales")
+                nc.vector.tensor_tensor(damped_first[:], weight[:, 0, 0:2], damping_first[:], MULT)
 
         vals = keep.tile([P, SLOTS], U32, name="vals", align_bytes=64)
         for h in range(2):
             gather(vals, val_pool[:].bitcast(U32), h * HALF, (h + 1) * HALF)
 
-        damped_rest = keep.tile([P, BLOCKS - 1, TILES, P], F32, name="damped_rest", tag="val_pool", align_bytes=64)
-        damped = [damped_first[:]] + [damped_rest[:, b] for b in range(BLOCKS - 1)]
-        for b in range(1, BLOCKS):
-            nc.vector.tensor_tensor(damped[b], weight[:, b], damping[:, b], MULT)
+        damped_rest = keep.tile([P, 3, 2, HALF], F32, name="damped_rest", tag="val_pool", align_bytes=64)
+        damped = [damped_first[:]] + [damped_rest[:, n] for n in range(3)]
+        for n in range(1, 4):
+            h, pair = parts[n]
+            tiles = slice(2 * pair, 2 * pair + 2)
+            nc.vector.tensor_tensor(damped[n], weight[:, h, tiles], damping[:, h, tiles], MULT)
 
         squares = []
-        for b in range(BLOCKS):
-            slots = slice(b * P, (b + 1) * P)
-            grads = psum.tile([P, TILES, P], F32, name="grads", tag="grads", bufs=4)
-            for j in range(TILES):
-                cols = slice(j * P, (j + 1) * P)
-                nc.tensor.matmul_mx(
-                    grads[:, j, :],
-                    lhsT=gout_codes[:, cols].bitcast(FP8X4),
-                    lhsT_scale=gout_scales[:, cols],
-                    rhs=vals[:, slots].bitcast(FP8X4),
-                    rhs_scale=val_scales[VALS_SCALE_ROW:P, slots],
-                    start=True,
-                    stop=True,
-                )
-            square = keep.tile([P, TILES, P], F32, name="square", tag="square", bufs=4)
+        for h, pair in parts:
+            grads = multiply("grads", gout_codes, gout_scales, vals, val_scales[VALS_SCALE_ROW:P, :], h, pair)
+            square = keep.tile([P, 2, HALF], F32, name="square", tag="square", bufs=4)
             nc.scalar.activation(square[:], grads[:], ACT.Square)
             squares.append(square)
 
-        sums = []
+        totals = [psum.tile([P, P], F32, name="total", tag="early", bufs=4) for b in range(BLOCKS)]
 
-        def finish(b):
-            pairs = sums[b][:].rearrange("p (g h) -> p h g", h=2)
-            partial = keep.tile([P, GROUPS], F32, name="partial", tag="partial", bufs=4)
+        def add_turned(curvature, n, i, side):
+            h, pair = parts[n]
+            j = 2 * pair + i
+            nc.tensor.matmul(
+                totals[2 * h + side][:],
+                curvature[:, i, side * P : (side + 1) * P],
+                identity[:],
+                start=(j == 0),
+                stop=(j == TILES - 1),
+                is_transpose=True,
+            )
+
+        for n in range(4):
+            curvature = keep.tile([P, 2, HALF], F32, name="curvature", tag="curvature", bufs=4)
+            if n < 3:
+                nc.vector.tensor_tensor(curvature[:], damped[n], squares[n][:], MULT)
+            for side in range(2):
+                cols = slice(side * P, (side + 1) * P)
+                if n == 3:
+                    nc.vector.tensor_tensor(curvature[:, :, cols], damped[n][:, :, cols], squares[n][:, :, cols], MULT)
+                for i in range(2):
+                    add_turned(curvature, n, i, side)
+
+        partials = keep.tile([P, BLOCKS, GROUPS], F32, name="partials", tag="val_pool", align_bytes=64)
+        for b in range(BLOCKS):
+            pairs = totals[b][:].rearrange("p (g h) -> p h g", h=2)
             nc.vector.scalar_tensor_tensor(
-                partial[:], old_rows[:, b, :], fade_cols[:, b : b + 1], pairs[:, 0, :], MULT, ADD
+                partials[:, b, :], old_rows[:, b, :], fade_cols[:, b : b + 1], pairs[:, 0, :], MULT, ADD
             )
             result = keep.tile([P, GROUPS], F32, name="result", tag="result", bufs=4)
-            nc.vector.tensor_tensor(result[:], pairs[:, 1, :], partial[:], ADD)
+            nc.vector.tensor_tensor(result[:], pairs[:, 1, :], partials[:, b, :], ADD)
             nc.sync.dma_start(out[b * P : (b + 1) * P, :], result[:])
-
-        for b in range(BLOCKS):
-            curvature = keep.tile([P, TILES, P], F32, name="curvature", tag="curvature", bufs=4)
-            step = TILES if b < BLOCKS - 1 else 1
-            for j in range(0, TILES, step):
-                tiles = slice(j, j + step)
-                nc.vector.tensor_tensor(curvature[:, tiles], damped[b][:, tiles], squares[b][:, tiles], MULT)
-            total = psum.tile([P, P], F32, name="total", tag="early", bufs=4)
-            for j in range(TILES):
-                nc.tensor.matmul(
-                    total[:], curvature[:, j, :], identity[:], start=(j == 0), stop=(j == TILES - 1), is_transpose=True
-                )
-            sums.append(total)
-            if b >= 1:
-                finish(b - 1)
-        finish(BLOCKS - 1)

@@ -37,8 +37,9 @@ def tile_attend_curvatures_kernel(
         nc.sync.dma_start(offsets[:], offs)
         lse_cols = keep.tile([P, TILES], F32, name="lse_cols")
         nc.sync.dma_start(lse_cols[:], lse.rearrange("o (p j) -> (o p) j", j=TILES))
-        mult_cols = keep.tile([P, TILES], F32, name="mult_cols")
-        nc.sync.dma_start(mult_cols[:], mult.rearrange("o (p j) -> (o p) j", j=TILES))
+        query_rows = query.rearrange("(p t) q -> p t q", t=PACK)
+        query_raw = keep.tile([P, PACK, Q], F32, name="query_raw")
+        nc.sync.dma_start(query_raw[:, 0:1, :], query_rows[:, 0:1, :])
 
         def load_scale_rows(name, scales, first_row, zero_engine, queues):
             pool_rows = keep.tile([P, T], U8, name=name, tag=name, align_bytes=64)
@@ -61,15 +62,17 @@ def tile_attend_curvatures_kernel(
         key_scale_pool = load_scale_rows(
             "key_scale_pool", keys_scales, 0, nc.vector, [nc.sync, nc.sync, nc.scalar, nc.scalar]
         )
-        query_raw = load_rows("query_raw", query, 0, Q)
+        nc.sync.dma_start(query_raw[:, 1:PACK, :], query_rows[:, 1:PACK, :])
         val_scale_pool = load_scale_rows("val_scale_pool", vals_scales, VALS_SCALE_ROW, nc.gpsimd, [nc.sync] * 4)
         key_pool = load_words("key_pool", keys_words)
+        mult_cols = keep.tile([P, TILES], F32, name="mult_cols")
+        nc.sync.dma_start(mult_cols[:], mult.rearrange("o (p j) -> (o p) j", j=TILES))
         gout_raw0 = load_rows("gout_raw0", gout, 0, Q // 2)
         gout_raw1 = load_rows("gout_raw1", gout, Q // 2, Q)
         val_pool = load_words("val_pool", vals_words)
 
         neg_lse = keep.tile([P, TILES], F32, name="neg_lse")
-        nc.gpsimd.tensor_scalar(neg_lse[:], lse_cols[:], -1.0, 0.0, MULT, ADD)
+        nc.scalar.activation(neg_lse[:], lse_cols[:], ACT.Copy, scale=-1.0)
         slope = keep.tile([P, TILES], F32, name="slope")
         nc.gpsimd.tensor_scalar(slope[:], mult_cols[:], -512.0, 0.0, MULT, ADD)
         identity = keep.tile([P, P], F32, name="identity")
@@ -204,11 +207,12 @@ def tile_attend_curvatures_kernel(
                     add_turned(curvature, n, i, side)
 
         partials = keep.tile([P, BLOCKS, GROUPS], F32, name="partials", tag="val_pool", align_bytes=64)
+        halves = [totals[b][:].rearrange("p (g e) -> p e g", e=2) for b in range(BLOCKS)]
         for b in range(BLOCKS):
-            pairs = totals[b][:].rearrange("p (g h) -> p h g", h=2)
             nc.vector.scalar_tensor_tensor(
-                partials[:, b, :], old_rows[:, b, :], fade_cols[:, b : b + 1], pairs[:, 0, :], MULT, ADD
+                partials[:, b, :], old_rows[:, b, :], fade_cols[:, b : b + 1], halves[b][:, 0, :], MULT, ADD
             )
+        for b in range(BLOCKS):
             result = keep.tile([P, GROUPS], F32, name="result", tag="result", bufs=4)
-            nc.vector.tensor_tensor(result[:], pairs[:, 1, :], partials[:, b, :], ADD)
+            nc.vector.tensor_tensor(result[:], halves[b][:, 1, :], partials[:, b, :], ADD)
             nc.sync.dma_start(out[b * P : (b + 1) * P, :], result[:])

@@ -3,8 +3,9 @@ from contextlib import ExitStack
 import concourse.mybir as mybir
 from concourse.masks import make_identity
 
-D, T, SLOTS, Q, GROUPS = 512, 2048, 512, 512, 64
-FLOPS = 2 * 2 * D * SLOTS * Q
+K, TOKENS, SLOTS, Q, GROUPS = 512, 2048, 512, 512, 64
+FLOPS = 2 * 2 * K * SLOTS * Q
+GAIN = 512.0
 
 F32 = mybir.dt.float32
 BF16 = mybir.dt.bfloat16
@@ -19,10 +20,15 @@ ADD = mybir.AluOpType.add
 
 P = 128
 PACK = 4
-TILES = Q // P
-BLOCKS = SLOTS // P
+QUADRANT = 32
+LIST_ROWS = 16
+ROW_TILES = Q // P
+SLOT_BLOCKS = SLOTS // P
 HALF = SLOTS // 2
-VALS_SCALE_ROW = 4
+PARTS = [(half, pair) for half in range(2) for pair in range(2)]
+BANKS = len(PARTS)
+VAL_SCALE_ROW = 4
+MX_ALIGN = 64
 
 
 def tile_attend_curvatures_kernel(
@@ -33,186 +39,193 @@ def tile_attend_curvatures_kernel(
         keep = ctx.enter_context(tc.tile_pool(name="keep", bufs=1))
         psum = ctx.enter_context(tc.psum_pool(name="psum", bufs=1))
 
-        offsets = keep.tile([P, SLOTS // 16], U16, name="offsets")
-        nc.sync.dma_start(offsets[:], offs)
-        lse_cols = keep.tile([P, TILES], F32, name="lse_cols")
-        nc.sync.dma_start(lse_cols[:], lse.rearrange("o (p j) -> (o p) j", j=TILES))
-        query_rows = query.rearrange("(p t) q -> p t q", t=PACK)
-        query_raw = keep.tile([P, PACK, Q], F32, name="query_raw")
-        nc.sync.dma_start(query_raw[:, 0:1, :], query_rows[:, 0:1, :])
-
-        def load_scale_rows(name, scales, first_row, zero_engine, queues):
-            pool_rows = keep.tile([P, T], U8, name=name, tag=name, align_bytes=64)
-            zero_engine.memset(pool_rows[:].bitcast(I32), 0)
-            rows = scales[0].bitcast(I32).rearrange("(quad r) c -> r quad c", r=4)
-            for r, queue in enumerate(queues):
-                queue.dma_start(pool_rows[first_row + r : P : 32, :].bitcast(I32), rows[r])
+        def load_scale_rows(name, scales, first_row):
+            pool_rows = keep.tile([P, TOKENS], U8, name=name, tag=name, align_bytes=MX_ALIGN)
+            nc.vector.memset(pool_rows[:].bitcast(I32), 0)
+            rows = scales[0].bitcast(I32).rearrange("(c r) n -> r c n", r=4)
+            for r in range(4):
+                nc.sync.dma_start(pool_rows[first_row + r : P : QUADRANT, :].bitcast(I32), rows[r])
             return pool_rows
 
         def load_words(name, words):
-            pool_words = keep.tile([P, T], I32, name=name, tag=name, align_bytes=64)
+            pool_words = keep.tile([P, TOKENS], I32, name=name, tag=name, align_bytes=MX_ALIGN)
             nc.sync.dma_start(pool_words[:], words[0].rearrange("p n t -> p (n t)").bitcast(I32))
             return pool_words
 
-        def load_rows(name, matrix, c0, c1):
-            raw = keep.tile([P, PACK, c1 - c0], F32, name=name, tag=name)
-            nc.sync.dma_start(raw[:], matrix[:, c0:c1].rearrange("(p t) q -> p t q", t=PACK))
+        def load_row_vector(name, vector):
+            cols = keep.tile([P, ROW_TILES], F32, name=name, tag=name)
+            nc.sync.dma_start(cols[:], vector.rearrange("o (m j) -> (o m) j", j=ROW_TILES))
+            return cols
+
+        def load_gout_half(name, half):
+            raw = keep.tile([P, PACK, Q // 2], F32, name=name, tag=name)
+            columns = gout[:, half * Q // 2 : (half + 1) * Q // 2]
+            nc.sync.dma_start(raw[:], columns.rearrange("(p t) q -> p t q", t=PACK))
             return raw
 
-        key_scale_pool = load_scale_rows(
-            "key_scale_pool", keys_scales, 0, nc.vector, [nc.sync, nc.sync, nc.scalar, nc.scalar]
-        )
-        nc.sync.dma_start(query_raw[:, 1:PACK, :], query_rows[:, 1:PACK, :])
-        val_scale_pool = load_scale_rows("val_scale_pool", vals_scales, VALS_SCALE_ROW, nc.gpsimd, [nc.sync] * 4)
-        key_pool = load_words("key_pool", keys_words)
-        mult_cols = keep.tile([P, TILES], F32, name="mult_cols")
-        nc.sync.dma_start(mult_cols[:], mult.rearrange("o (p j) -> (o p) j", j=TILES))
-        gout_raw0 = load_rows("gout_raw0", gout, 0, Q // 2)
-        gout_raw1 = load_rows("gout_raw1", gout, Q // 2, Q)
-        val_pool = load_words("val_pool", vals_words)
-
-        neg_lse = keep.tile([P, TILES], F32, name="neg_lse")
-        nc.scalar.activation(neg_lse[:], lse_cols[:], ACT.Copy, scale=-1.0)
-        slope = keep.tile([P, TILES], F32, name="slope")
-        nc.gpsimd.tensor_scalar(slope[:], mult_cols[:], -512.0, 0.0, MULT, ADD)
-        identity = keep.tile([P, P], F32, name="identity")
-        make_identity(nc, identity[:])
-
-        def interleave(copy, woven, raw, j0, j1, m0, m1):
+        def weave(copy, woven, raw, pair, m0, m1):
+            tiles = slice(2 * pair, 2 * pair + 2)
             copy(
-                woven[:, j0:j1, m0:m1, :].rearrange("p j m t -> p m t j"),
-                raw[:].rearrange("p t (m j) -> p m t j", j=TILES)[:, :, :, j0:j1],
+                woven[:, tiles, m0:m1, :].rearrange("p j m t -> p m t j"),
+                raw[:].rearrange("p t (m j) -> p m t j", j=ROW_TILES)[:, :, :, tiles],
             )
 
-        def gather(gathered, pool_ap, s0, s1):
-            nc.vector.tensor_copy(gathered[:, s0:s1], pool_ap.indirect(offsets[:, s0 // 16 : s1 // 16]))
-
-        key_scales = keep.tile([P, SLOTS], U8, name="key_scales", align_bytes=64)
-        gather(key_scales, key_scale_pool[:], 0, SLOTS)
-
-        query_woven = keep.tile([P, TILES, P, PACK], BF16, name="query_woven", align_bytes=64)
-        interleave(nc.vector.tensor_copy, query_woven, query_raw, 0, 2, 0, P)
-        interleave(nc.scalar.copy, query_woven, query_raw, 2, 4, 0, P)
-
-        val_scales = keep.tile([P, SLOTS], U8, name="val_scales", align_bytes=64)
-        gather(val_scales, val_scale_pool[:], 0, SLOTS)
-
         def quantize(name, woven, scale_tag):
-            codes = keep.tile([P, Q], U32, name=name + "_codes", align_bytes=64)
-            scales = keep.tile([P, Q], U8, name=name + "_scales", tag=scale_tag, align_bytes=64)
+            codes = keep.tile([P, Q], U32, name=name + "_codes", align_bytes=MX_ALIGN)
+            scales = keep.tile([P, Q], U8, name=name + "_scales", tag=scale_tag, align_bytes=MX_ALIGN)
             nc.vector.quantize_mx(
                 out=codes[:].bitcast(FP8X4), scales=scales[:], in_=woven[:].rearrange("p j m t -> p (j m t)")
             )
             return codes, scales
 
-        query_codes, query_scales = quantize("query", query_woven, "val_scale_pool")
+        def gather(gathered, window, s0, s1):
+            nc.vector.tensor_copy(gathered[:, s0:s1], window.indirect(offsets[:, s0 // LIST_ROWS : s1 // LIST_ROWS]))
 
-        gout_woven = keep.tile([P, TILES, P, PACK], BF16, name="gout_woven", align_bytes=64)
-
-        old_rows = keep.tile([P, BLOCKS, GROUPS], F32, name="old_rows")
-        nc.sync.dma_start(old_rows[:], old.rearrange("(b p) g -> p b g", p=P))
-        fade_cols = keep.tile([P, BLOCKS], F32, name="fade_cols")
-        with nc.allow_non_contiguous_dma(reason="one value of fade for each partition and block"):
-            nc.sync.dma_start(fade_cols[:], fade.rearrange("(b p) o -> p (b o)", p=P))
-
-        keys = keep.tile([P, SLOTS], U32, name="keys", align_bytes=64)
-        for h in range(2):
-            gather(keys, key_pool[:].bitcast(U32), h * HALF, (h + 1) * HALF)
-        for j0 in (0, 2):
-            interleave(nc.vector.tensor_copy, gout_woven, gout_raw0, j0, j0 + 2, 0, P // 2)
-        for j0 in (0, 2):
-            interleave(nc.vector.tensor_copy, gout_woven, gout_raw1, j0, j0 + 2, P // 2, P)
-
-        def multiply(tag, codes, scales, columns, column_scales, h, pair):
-            slots = slice(h * HALF, (h + 1) * HALF)
-            bank = psum.tile([P, 2, HALF], F32, name=tag, tag=tag, bufs=4)
+        def multiply(tag, row_codes, row_scales, slot_codes, slot_scales, half, pair):
+            slots = slice(half * HALF, (half + 1) * HALF)
+            bank = psum.tile([P, 2, HALF], F32, name=tag, tag=tag, bufs=BANKS)
             for i in range(2):
                 rows = slice((2 * pair + i) * P, (2 * pair + i + 1) * P)
                 nc.tensor.matmul_mx(
                     bank[:, i, :],
-                    lhsT=codes[:, rows].bitcast(FP8X4),
-                    lhsT_scale=scales[:, rows],
-                    rhs=columns[:, slots].bitcast(FP8X4),
-                    rhs_scale=column_scales[:, slots],
+                    lhsT=row_codes[:, rows].bitcast(FP8X4),
+                    lhsT_scale=row_scales[:, rows],
+                    rhs=slot_codes[:, slots].bitcast(FP8X4),
+                    rhs_scale=slot_scales[:, slots],
                     start=True,
                     stop=True,
                 )
             return bank
 
-        parts = [(h, pair) for h in range(2) for pair in range(2)]
-        weight = keep.tile([P, 2, TILES, HALF], F32, name="weight")
-        damping = keep.tile([P, 2, TILES, HALF], F32, name="damping")
-        damping_first = keep.tile([P, 2, HALF], F32, name="damping_first", tag="gout_raw1")
-        damped_first = keep.tile([P, 2, HALF], F32, name="damped_first")
-        for h in range(2):
+        offsets = keep.tile([P, SLOTS // LIST_ROWS], U16, name="offsets")
+        nc.sync.dma_start(offsets[:], offs)
+        lse_cols = load_row_vector("lse_cols", lse)
+        query_rows = query.rearrange("(p t) q -> p t q", t=PACK)
+        query_raw = keep.tile([P, PACK, Q], F32, name="query_raw")
+        nc.sync.dma_start(query_raw[:, 0:1, :], query_rows[:, 0:1, :])
+        key_scale_pool = load_scale_rows("key_scale_pool", keys_scales, 0)
+        nc.sync.dma_start(query_raw[:, 1:PACK, :], query_rows[:, 1:PACK, :])
+        val_scale_pool = load_scale_rows("val_scale_pool", vals_scales, VAL_SCALE_ROW)
+        key_pool = load_words("key_pool", keys_words)
+        mult_cols = load_row_vector("mult_cols", mult)
+        gout_raw = [load_gout_half("gout_raw0", 0), load_gout_half("gout_raw1", 1)]
+        val_pool = load_words("val_pool", vals_words)
+
+        neg_lse = keep.tile([P, ROW_TILES], F32, name="neg_lse")
+        nc.scalar.activation(neg_lse[:], lse_cols[:], ACT.Copy, scale=-1.0)
+        identity = keep.tile([P, P], F32, name="identity", tag="lse_cols")
+        make_identity(nc, identity[:])
+
+        key_scales = keep.tile([P, SLOTS], U8, name="key_scales", align_bytes=MX_ALIGN)
+        gather(key_scales, key_scale_pool[:], 0, SLOTS)
+
+        query_woven = keep.tile([P, ROW_TILES, P, PACK], BF16, name="query_woven", align_bytes=MX_ALIGN)
+        weave(nc.vector.tensor_copy, query_woven, query_raw, 0, 0, P)
+        weave(nc.scalar.copy, query_woven, query_raw, 1, 0, P)
+
+        val_scales = keep.tile([P, SLOTS], U8, name="val_scales", align_bytes=MX_ALIGN)
+        gather(val_scales, val_scale_pool[:], 0, SLOTS)
+        query_codes, query_scales = quantize("query", query_woven, "val_scale_pool")
+
+        slope = keep.tile([P, ROW_TILES], F32, name="slope")
+        nc.scalar.activation(slope[:], mult_cols[:], ACT.Copy, scale=-GAIN)
+
+        old_rows = keep.tile([P, SLOT_BLOCKS, GROUPS], F32, name="old_rows")
+        nc.sync.dma_start(old_rows[:], old.rearrange("(b p) g -> p b g", p=P))
+        fade_cols = keep.tile([P, SLOT_BLOCKS], F32, name="fade_cols")
+        with nc.allow_non_contiguous_dma(reason="one value of fade for each partition and slot block"):
+            nc.sync.dma_start(fade_cols[:], fade.rearrange("(b p) o -> p (b o)", p=P))
+
+        keys = keep.tile([P, SLOTS], U32, name="keys", align_bytes=MX_ALIGN)
+        for half in range(2):
+            gather(keys, key_pool[:].bitcast(U32), half * HALF, (half + 1) * HALF)
+        gout_woven = keep.tile([P, ROW_TILES, P, PACK], BF16, name="gout_woven", align_bytes=MX_ALIGN)
+        for side in range(2):
             for pair in range(2):
-                scores = multiply("early", query_codes, query_scales, keys, key_scales[:], h, pair)
+                weave(nc.vector.tensor_copy, gout_woven, gout_raw[side], pair, side * P // 2, (side + 1) * P // 2)
+
+        weight = keep.tile([P, BANKS, 2, HALF], F32, name="weight")
+        damping_first = keep.tile([P, 2, HALF], F32, name="damping_first", tag="gout_raw1")
+        damping_rest = keep.tile([P, BANKS - 1, 2, HALF], F32, name="damping_rest")
+        damping = [damping_first[:]] + [damping_rest[:, n] for n in range(BANKS - 1)]
+
+        def exponentials(half):
+            for pair in range(2):
+                scores = multiply("scores", query_codes, query_scales, keys, key_scales[:], half, pair)
                 for i in range(2):
                     j = 2 * pair + i
-                    nc.scalar.activation(weight[:, h, j, :], scores[:, i, :], ACT.Exp, bias=neg_lse[:, j : j + 1])
-            for j in range(TILES):
-                if h == 0 and j < 2:
-                    nc.vector.tensor_scalar(
-                        damping_first[:, j, :], weight[:, h, j, :], slope[:, j : j + 1], 512.0, MULT, ADD
-                    )
-                else:
                     nc.scalar.activation(
-                        damping[:, h, j, :], weight[:, h, j, :], ACT.Copy, bias=512.0, scale=slope[:, j : j + 1]
+                        weight[:, 2 * half + pair, i, :], scores[:, i, :], ACT.Exp, bias=neg_lse[:, j : j + 1]
                     )
-            if h == 0:
-                gout_codes, gout_scales = quantize("gout", gout_woven, "gout_scales")
-                nc.vector.tensor_tensor(damped_first[:], weight[:, 0, 0:2], damping_first[:], MULT)
 
-        vals = keep.tile([P, SLOTS], U32, name="vals", align_bytes=64)
-        for h in range(2):
-            gather(vals, val_pool[:].bitcast(U32), h * HALF, (h + 1) * HALF)
+        def damp_on_scalar(n):
+            for i in range(2):
+                j = 2 * PARTS[n][1] + i
+                nc.scalar.activation(
+                    damping[n][:, i, :], weight[:, n, i, :], ACT.Copy, bias=GAIN, scale=slope[:, j : j + 1]
+                )
 
-        damped_rest = keep.tile([P, 3, 2, HALF], F32, name="damped_rest", tag="val_pool", align_bytes=64)
-        damped = [damped_first[:]] + [damped_rest[:, n] for n in range(3)]
-        for n in range(1, 4):
-            h, pair = parts[n]
-            tiles = slice(2 * pair, 2 * pair + 2)
-            nc.vector.tensor_tensor(damped[n], weight[:, h, tiles], damping[:, h, tiles], MULT)
+        exponentials(0)
+        for i in range(2):
+            nc.vector.tensor_scalar(damping[0][:, i, :], weight[:, 0, i, :], slope[:, i : i + 1], GAIN, MULT, ADD)
+        damp_on_scalar(1)
+        gout_codes, gout_scales = quantize("gout", gout_woven, "gout_scales")
+        damped_first = keep.tile([P, 2, HALF], F32, name="damped_first")
+        nc.vector.tensor_tensor(damped_first[:], weight[:, 0], damping[0], MULT)
+        exponentials(1)
+        damp_on_scalar(2)
+        damp_on_scalar(3)
+
+        vals = keep.tile([P, SLOTS], U32, name="vals", align_bytes=MX_ALIGN)
+        for half in range(2):
+            gather(vals, val_pool[:].bitcast(U32), half * HALF, (half + 1) * HALF)
+
+        damped_rest = keep.tile([P, BANKS - 1, 2, HALF], F32, name="damped_rest", tag="val_pool", align_bytes=MX_ALIGN)
+        damped = [damped_first[:]] + [damped_rest[:, n] for n in range(BANKS - 1)]
+        for n in range(1, BANKS):
+            nc.vector.tensor_tensor(damped[n], weight[:, n], damping[n], MULT)
 
         squares = []
-        for h, pair in parts:
-            grads = multiply("grads", gout_codes, gout_scales, vals, val_scales[VALS_SCALE_ROW:P, :], h, pair)
-            square = keep.tile([P, 2, HALF], F32, name="square", tag="square", bufs=4)
+        for half, pair in PARTS:
+            grads = multiply("grads", gout_codes, gout_scales, vals, val_scales[VAL_SCALE_ROW:P, :], half, pair)
+            square = keep.tile([P, 2, HALF], F32, name="square", tag="square", bufs=BANKS)
             nc.scalar.activation(square[:], grads[:], ACT.Square)
             squares.append(square)
 
-        totals = [psum.tile([P, P], F32, name="total", tag="early", bufs=4) for b in range(BLOCKS)]
+        totals = [psum.tile([P, P], F32, name="total", tag="scores", bufs=BANKS) for b in range(SLOT_BLOCKS)]
 
-        def add_turned(curvature, n, i, side):
-            h, pair = parts[n]
-            j = 2 * pair + i
-            nc.tensor.matmul(
-                totals[2 * h + side][:],
-                curvature[:, i, side * P : (side + 1) * P],
-                identity[:],
-                start=(j == 0),
-                stop=(j == TILES - 1),
-                is_transpose=True,
-            )
+        def add_turned(curvature, n, side):
+            half, pair = PARTS[n]
+            for i in range(2):
+                j = 2 * pair + i
+                nc.tensor.matmul(
+                    totals[2 * half + side][:],
+                    curvature[:, i, side * P : (side + 1) * P],
+                    identity[:],
+                    start=(j == 0),
+                    stop=(j == ROW_TILES - 1),
+                    is_transpose=True,
+                )
 
-        for n in range(4):
-            curvature = keep.tile([P, 2, HALF], F32, name="curvature", tag="curvature", bufs=4)
-            if n < 3:
-                nc.vector.tensor_tensor(curvature[:], damped[n], squares[n][:], MULT)
+        for n in range(BANKS - 1):
+            curvature = keep.tile([P, 2, HALF], F32, name="curvature", tag="curvature", bufs=BANKS)
+            nc.vector.tensor_tensor(curvature[:], damped[n], squares[n][:], MULT)
             for side in range(2):
-                cols = slice(side * P, (side + 1) * P)
-                if n == 3:
-                    nc.vector.tensor_tensor(curvature[:, :, cols], damped[n][:, :, cols], squares[n][:, :, cols], MULT)
-                for i in range(2):
-                    add_turned(curvature, n, i, side)
+                add_turned(curvature, n, side)
+        last = BANKS - 1
+        curvature = keep.tile([P, 2, HALF], F32, name="curvature", tag="curvature", bufs=BANKS)
+        for side in range(2):
+            cols = slice(side * P, (side + 1) * P)
+            nc.vector.tensor_tensor(curvature[:, :, cols], damped[last][:, :, cols], squares[last][:, :, cols], MULT)
+            add_turned(curvature, last, side)
 
-        partials = keep.tile([P, BLOCKS, GROUPS], F32, name="partials", tag="val_pool", align_bytes=64)
-        halves = [totals[b][:].rearrange("p (g e) -> p e g", e=2) for b in range(BLOCKS)]
-        for b in range(BLOCKS):
+        partials = keep.tile([P, SLOT_BLOCKS, GROUPS], F32, name="partials", tag="val_pool", align_bytes=MX_ALIGN)
+        by_parity = [total[:].rearrange("p (g e) -> p e g", e=2) for total in totals]
+        for b in range(SLOT_BLOCKS):
             nc.vector.scalar_tensor_tensor(
-                partials[:, b, :], old_rows[:, b, :], fade_cols[:, b : b + 1], halves[b][:, 0, :], MULT, ADD
+                partials[:, b, :], old_rows[:, b, :], fade_cols[:, b : b + 1], by_parity[b][:, 0, :], MULT, ADD
             )
-        for b in range(BLOCKS):
-            result = keep.tile([P, GROUPS], F32, name="result", tag="result", bufs=4)
-            nc.vector.tensor_tensor(result[:], halves[b][:, 1, :], partials[:, b, :], ADD)
+        for b in range(SLOT_BLOCKS):
+            result = keep.tile([P, GROUPS], F32, name="result", tag="result", bufs=SLOT_BLOCKS)
+            nc.vector.tensor_tensor(result[:], by_parity[b][:, 1, :], partials[:, b, :], ADD)
             nc.sync.dma_start(out[b * P : (b + 1) * P, :], result[:])

from contextlib import ExitStack

import concourse.mybir as mybir
from concourse.masks import make_identity

K, TOKENS, SLOTS, Q, GROUPS = 512, 2048, 512, 512, 64
FLOPS = 2 * 2 * K * SLOTS * Q
GAIN = 512.0

F32 = mybir.dt.float32
BF16 = mybir.dt.bfloat16
I32 = mybir.dt.int32
U32 = mybir.dt.uint32
U16 = mybir.dt.uint16
U8 = mybir.dt.uint8
FP8X4 = mybir.dt.float8_e4m3fn_x4
ACT = mybir.ActivationFunctionType
MULT = mybir.AluOpType.mult
ADD = mybir.AluOpType.add

P = 128
PACK = 4
QUADRANT = 32
LIST_ROWS = 16
ROW_TILES = Q // P
SLOT_BLOCKS = SLOTS // P
HALF = SLOTS // 2
PARTS = [(half, pair) for half in range(2) for pair in range(2)]
BANKS = len(PARTS)
VAL_SCALE_ROW = 4
MX_ALIGN = 64


def tile_attend_curvatures_kernel(
    tc, query, keys_words, keys_scales, lse, mult, gout, vals_words, vals_scales, old, fade, offs, out
):
    nc = tc.nc
    with ExitStack() as ctx:
        keep = ctx.enter_context(tc.tile_pool(name="keep", bufs=1))
        psum = ctx.enter_context(tc.psum_pool(name="psum", bufs=1))

        def load_scale_rows(name, scales, first_row):
            pool_rows = keep.tile([P, TOKENS], U8, name=name, tag=name, align_bytes=MX_ALIGN)
            nc.vector.memset(pool_rows[:].bitcast(I32), 0)
            rows = scales[0].bitcast(I32).rearrange("(c r) n -> r c n", r=4)
            for r in range(4):
                nc.sync.dma_start(pool_rows[first_row + r : P : QUADRANT, :].bitcast(I32), rows[r])
            return pool_rows

        def load_words(name, words):
            pool_words = keep.tile([P, TOKENS], I32, name=name, tag=name, align_bytes=MX_ALIGN)
            nc.sync.dma_start(pool_words[:], words[0].rearrange("p n t -> p (n t)").bitcast(I32))
            return pool_words

        def load_row_vector(name, vector):
            cols = keep.tile([P, ROW_TILES], F32, name=name, tag=name)
            nc.sync.dma_start(cols[:], vector.rearrange("o (m j) -> (o m) j", j=ROW_TILES))
            return cols

        def load_gout_half(name, half):
            raw = keep.tile([P, PACK, Q // 2], F32, name=name, tag=name)
            columns = gout[:, half * Q // 2 : (half + 1) * Q // 2]
            nc.sync.dma_start(raw[:], columns.rearrange("(p t) q -> p t q", t=PACK))
            return raw

        def weave(copy, woven, raw, pair, m0, m1):
            tiles = slice(2 * pair, 2 * pair + 2)
            copy(
                woven[:, tiles, m0:m1, :].rearrange("p j m t -> p m t j"),
                raw[:].rearrange("p t (m j) -> p m t j", j=ROW_TILES)[:, :, :, tiles],
            )

        def quantize(name, woven, scale_tag):
            codes = keep.tile([P, Q], U32, name=name + "_codes", align_bytes=MX_ALIGN)
            scales = keep.tile([P, Q], U8, name=name + "_scales", tag=scale_tag, align_bytes=MX_ALIGN)
            nc.vector.quantize_mx(
                out=codes[:].bitcast(FP8X4), scales=scales[:], in_=woven[:].rearrange("p j m t -> p (j m t)")
            )
            return codes, scales

        def gather(gathered, window, s0, s1):
            nc.vector.tensor_copy(gathered[:, s0:s1], window.indirect(offsets[:, s0 // LIST_ROWS : s1 // LIST_ROWS]))

        def multiply(tag, row_codes, row_scales, slot_codes, slot_scales, half, pair):
            slots = slice(half * HALF, (half + 1) * HALF)
            bank = psum.tile([P, 2, HALF], F32, name=tag, tag=tag, bufs=BANKS)
            for i in range(2):
                rows = slice((2 * pair + i) * P, (2 * pair + i + 1) * P)
                nc.tensor.matmul_mx(
                    bank[:, i, :],
                    lhsT=row_codes[:, rows].bitcast(FP8X4),
                    lhsT_scale=row_scales[:, rows],
                    rhs=slot_codes[:, slots].bitcast(FP8X4),
                    rhs_scale=slot_scales[:, slots],
                    start=True,
                    stop=True,
                )
            return bank

        offsets = keep.tile([P, SLOTS // LIST_ROWS], U16, name="offsets")
        nc.sync.dma_start(offsets[:], offs)
        lse_cols = load_row_vector("lse_cols", lse)
        query_rows = query.rearrange("(p t) q -> p t q", t=PACK)
        query_raw = keep.tile([P, PACK, Q], F32, name="query_raw")
        nc.sync.dma_start(query_raw[:, 0:1, :], query_rows[:, 0:1, :])
        key_scale_pool = load_scale_rows("key_scale_pool", keys_scales, 0)
        nc.sync.dma_start(query_raw[:, 1:PACK, :], query_rows[:, 1:PACK, :])
        val_scale_pool = load_scale_rows("val_scale_pool", vals_scales, VAL_SCALE_ROW)
        key_pool = load_words("key_pool", keys_words)
        mult_cols = load_row_vector("mult_cols", mult)
        gout_raw = [load_gout_half("gout_raw0", 0), load_gout_half("gout_raw1", 1)]
        val_pool = load_words("val_pool", vals_words)

        neg_lse = keep.tile([P, ROW_TILES], F32, name="neg_lse")
        nc.scalar.activation(neg_lse[:], lse_cols[:], ACT.Copy, scale=-1.0)
        identity = keep.tile([P, P], F32, name="identity", tag="lse_cols")
        make_identity(nc, identity[:])

        key_scales = keep.tile([P, SLOTS], U8, name="key_scales", align_bytes=MX_ALIGN)
        gather(key_scales, key_scale_pool[:], 0, SLOTS)

        query_woven = keep.tile([P, ROW_TILES, P, PACK], BF16, name="query_woven", align_bytes=MX_ALIGN)
        weave(nc.vector.tensor_copy, query_woven, query_raw, 0, 0, P)
        weave(nc.scalar.copy, query_woven, query_raw, 1, 0, P)

        val_scales = keep.tile([P, SLOTS], U8, name="val_scales", align_bytes=MX_ALIGN)
        gather(val_scales, val_scale_pool[:], 0, SLOTS)
        query_codes, query_scales = quantize("query", query_woven, "val_scale_pool")

        slope = keep.tile([P, ROW_TILES], F32, name="slope")
        nc.scalar.activation(slope[:], mult_cols[:], ACT.Copy, scale=-GAIN)

        old_rows = keep.tile([P, SLOT_BLOCKS, GROUPS], F32, name="old_rows")
        nc.sync.dma_start(old_rows[:], old.rearrange("(b p) g -> p b g", p=P))
        fade_cols = keep.tile([P, SLOT_BLOCKS], F32, name="fade_cols")
        with nc.allow_non_contiguous_dma(reason="one value of fade for each partition and slot block"):
            nc.sync.dma_start(fade_cols[:], fade.rearrange("(b p) o -> p (b o)", p=P))

        keys = keep.tile([P, SLOTS], U32, name="keys", align_bytes=MX_ALIGN)
        for half in range(2):
            gather(keys, key_pool[:].bitcast(U32), half * HALF, (half + 1) * HALF)
        gout_woven = keep.tile([P, ROW_TILES, P, PACK], BF16, name="gout_woven", align_bytes=MX_ALIGN)
        for side in range(2):
            for pair in range(2):
                weave(nc.vector.tensor_copy, gout_woven, gout_raw[side], pair, side * P // 2, (side + 1) * P // 2)

        weight = keep.tile([P, BANKS, 2, HALF], F32, name="weight")
        damping_first = keep.tile([P, 2, HALF], F32, name="damping_first", tag="gout_raw1")
        damping_rest = keep.tile([P, BANKS - 1, 2, HALF], F32, name="damping_rest")
        damping = [damping_first[:]] + [damping_rest[:, n] for n in range(BANKS - 1)]

        def exponentials(half):
            for pair in range(2):
                scores = multiply("scores", query_codes, query_scales, keys, key_scales[:], half, pair)
                for i in range(2):
                    j = 2 * pair + i
                    nc.scalar.activation(
                        weight[:, 2 * half + pair, i, :], scores[:, i, :], ACT.Exp, bias=neg_lse[:, j : j + 1]
                    )

        def damp_on_scalar(n):
            for i in range(2):
                j = 2 * PARTS[n][1] + i
                nc.scalar.activation(
                    damping[n][:, i, :], weight[:, n, i, :], ACT.Copy, bias=GAIN, scale=slope[:, j : j + 1]
                )

        exponentials(0)
        for i in range(2):
            nc.vector.tensor_scalar(damping[0][:, i, :], weight[:, 0, i, :], slope[:, i : i + 1], GAIN, MULT, ADD)
        damp_on_scalar(1)
        gout_codes, gout_scales = quantize("gout", gout_woven, "gout_scales")
        damped_first = keep.tile([P, 2, HALF], F32, name="damped_first")
        nc.vector.tensor_tensor(damped_first[:], weight[:, 0], damping[0], MULT)
        exponentials(1)
        damp_on_scalar(2)
        damp_on_scalar(3)

        vals = keep.tile([P, SLOTS], U32, name="vals", align_bytes=MX_ALIGN)
        for half in range(2):
            gather(vals, val_pool[:].bitcast(U32), half * HALF, (half + 1) * HALF)

        damped_rest = keep.tile([P, BANKS - 1, 2, HALF], F32, name="damped_rest", tag="val_pool", align_bytes=MX_ALIGN)
        damped = [damped_first[:]] + [damped_rest[:, n] for n in range(BANKS - 1)]
        for n in range(1, BANKS):
            nc.vector.tensor_tensor(damped[n], weight[:, n], damping[n], MULT)

        squares = []
        for half, pair in PARTS:
            grads = multiply("grads", gout_codes, gout_scales, vals, val_scales[VAL_SCALE_ROW:P, :], half, pair)
            square = keep.tile([P, 2, HALF], F32, name="square", tag="square", bufs=BANKS)
            nc.scalar.activation(square[:], grads[:], ACT.Square)
            squares.append(square)

        totals = [psum.tile([P, P], F32, name="total", tag="scores", bufs=BANKS) for b in range(SLOT_BLOCKS)]

        def add_turned(curvature, n, side):
            half, pair = PARTS[n]
            for i in range(2):
                j = 2 * pair + i
                nc.tensor.matmul(
                    totals[2 * half + side][:],
                    curvature[:, i, side * P : (side + 1) * P],
                    identity[:],
                    start=(j == 0),
                    stop=(j == ROW_TILES - 1),
                    is_transpose=True,
                )

        for n in range(BANKS - 1):
            curvature = keep.tile([P, 2, HALF], F32, name="curvature", tag="curvature", bufs=BANKS)
            nc.vector.tensor_tensor(curvature[:], damped[n], squares[n][:], MULT)
            for side in range(2):
                add_turned(curvature, n, side)
        last = BANKS - 1
        curvature = keep.tile([P, 2, HALF], F32, name="curvature", tag="curvature", bufs=BANKS)
        for side in range(2):
            cols = slice(side * P, (side + 1) * P)
            nc.vector.tensor_tensor(curvature[:, :, cols], damped[last][:, :, cols], squares[last][:, :, cols], MULT)
            add_turned(curvature, last, side)

        partials = keep.tile([P, SLOT_BLOCKS, GROUPS], F32, name="partials", tag="val_pool", align_bytes=MX_ALIGN)
        by_parity = [total[:].rearrange("p (g e) -> p e g", e=2) for total in totals]
        for b in range(SLOT_BLOCKS):
            nc.vector.scalar_tensor_tensor(
                partials[:, b, :], old_rows[:, b, :], fade_cols[:, b : b + 1], by_parity[b][:, 0, :], MULT, ADD
            )
        for b in range(SLOT_BLOCKS):
            result = keep.tile([P, GROUPS], F32, name="result", tag="result", bufs=SLOT_BLOCKS)
            nc.vector.tensor_tensor(result[:], by_parity[b][:, 1, :], partials[:, b, :], ADD)
            nc.sync.dma_start(out[b * P : (b + 1) * P, :], result[:])
